import numpy as np
import ml_dtypes


def mxq(x, axis, fmt="e4m3"):
    dtype, down = {"e4m3": (ml_dtypes.float8_e4m3fn, 7), "e5m2": (ml_dtypes.float8_e5m2, 14)}[fmt]
    v = np.moveaxis(np.asarray(x, np.float32).astype(ml_dtypes.bfloat16).astype(np.float64), axis, -1)
    blocks = v.reshape(v.shape[:-1] + (-1, 32))
    amax = np.abs(blocks).max(-1, keepdims=True)
    byte = np.maximum(np.where(amax > 0, np.frexp(amax)[1] - 1 + 127, 0) - down, 1)
    scale = np.exp2(byte - 127.0)
    codes = (blocks / scale).astype(np.float32).astype(dtype).astype(np.float64)
    return np.moveaxis((codes * scale).reshape(v.shape), -1, axis)


WIDE = False


def mx_kscale(k):
    if not WIDE:
        return np.ones(k)
    levels = np.array([10, -10, 5, -5, 0])
    if k % 512:
        return np.exp2(np.random.permutation(np.resize(levels, k // 32))).repeat(32)
    a = np.empty((k // 512, 16))
    for p in range(k // 512):
        a[p, :8] = np.random.permutation(np.resize(levels, 8))
        for g in range(8):
            far = levels[np.abs(levels - a[p, g]) >= 10]
            a[p, g + 8] = far[np.random.randint(len(far))]
    return np.exp2(a.ravel()).repeat(32)


def f64(x):
    return np.asarray(x).astype(np.float64)


def striped(idx):
    return np.tile(idx.reshape(-1, 16).T, (8, 1)).astype(np.uint16)


def unstriped(offs):
    return offs[:16].T.reshape(-1).astype(np.int64)


E2M1 = np.array([0.0, 0.5, 1.0, 1.5, 2.0, 3.0, 4.0, 6.0, -0.0, -0.5, -1.0, -1.5, -2.0, -3.0, -4.0, -6.0])


def pack_weight(w, fmt):
    k, n = w.shape
    w = f64(np.asarray(w, np.float32).astype(ml_dtypes.bfloat16)).reshape(k // 32, 32, n)
    amax = np.abs(w).max(1)
    if fmt == "e4m3":
        byte = np.frexp(amax)[1] - 1 + 127 - 7
    else:
        mant, ex = np.frexp(amax / 6.0)
        byte = np.where(mant > 0.5, ex, ex - 1) + 127
    byte = np.clip(np.where(amax > 0, byte, 1), 1, 254)
    scaled = (w * np.exp2(127.0 - byte)[:, None, :]).reshape(k, n).astype(np.float32)
    by_word = np.ascontiguousarray(scaled.reshape(k // 512, 128, 4, n).transpose(0, 1, 3, 2))
    if fmt == "e4m3":
        words = by_word.astype(ml_dtypes.float8_e4m3fn).view(np.uint8)
    else:
        c = by_word.astype(ml_dtypes.float4_e2m1fn).view(np.uint8) & 0xF
        words = (c[..., 0::2] | (c[..., 1::2] << 4)).reshape(k // 512, 128, 2 * n)
    return np.ascontiguousarray(words), np.ascontiguousarray(byte.astype(np.uint8).reshape(k // 512, 16, n))


def unpack_weight(words, scales, fmt):
    g, _, n = scales.shape
    words = np.ascontiguousarray(words).reshape(g, 128, n, -1)
    if fmt == "e4m3":
        vals = words.view(ml_dtypes.float8_e4m3fn).astype(np.float64)
    else:
        nib = np.empty((g, 128, n, 4), np.uint8)
        nib[..., 0::2] = words & 0xF
        nib[..., 1::2] = words >> 4
        vals = E2M1[nib]
    vals = vals * np.repeat(np.exp2(scales.astype(np.float64) - 127.0), 8, axis=1)[..., None]
    return vals.transpose(0, 1, 3, 2).reshape(g * 512, n)


def gelu(v):
    return 0.5 * v * (1.0 + np.tanh(np.sqrt(2.0 / np.pi) * (v + 0.044715 * v**3)))


K, T, E, C, H, N = 512, 1024, 16, 256, 512, 128
TOP = 4


def by_expert(wq, xq):
    return np.concatenate([wq[e].T @ xq[:, e * C:(e + 1) * C] for e in range(E)], axis=1)


def setup_inputs():
    n = np.random.standard_normal
    s = mx_kscale(K)[:, None]
    u = mx_kscale(H)
    deal = np.repeat(np.arange(E), C).reshape(TOP, T)[:, np.random.permutation(T)]
    deal = np.take_along_axis(deal, np.argsort(np.random.rand(TOP, T), axis=0), axis=0)
    for _ in range(8):
        s_, t_ = np.random.permutation(T).reshape(2, -1); r = np.random.randint(TOP, size=T // 2); x, y = deal[r, s_].copy(), deal[r, t_].copy()
        ok = ~((deal[:, s_] == y).any(0) | (deal[:, t_] == x).any(0)); deal[r[ok], s_[ok]] = y[ok]; deal[r[ok], t_[ok]] = x[ok]
    order = np.lexsort((np.random.rand(TOP * T), deal.reshape(-1)))
    slot_token = order % T; pos = np.empty(TOP * T, np.int64); pos[order] = np.arange(TOP * T); pos = pos.reshape(TOP, T)
    g = np.random.uniform(0.5, 1.5, (TOP, T)); g = g / g.sum(0)
    w1 = [pack_weight(m, "e2m1") for m in n((E, K, H)) / np.sqrt(K) / s[None] * u[None, None, :]]
    w2 = [pack_weight(m, "e2m1") for m in n((E, H, N)) / np.sqrt(H) / u[None, :, None]]
    return {
        "xT": (n((K, T)) * s).astype(np.float32),
        "w1_words": np.stack([m[0] for m in w1]),
        "w1_scales": np.stack([m[1] for m in w1]),
        "w2_words": np.stack([m[0] for m in w2]),
        "w2_scales": np.stack([m[1] for m in w2]),
        "gate": np.stack([np.tile(r, (N, 1)) for r in g]).astype(np.float32),
        "offs": striped(slot_token),
        "pos1": striped(pos[0]),
        "pos2": striped(pos[1]),
        "pos3": striped(pos[2]),
        "pos4": striped(pos[3]),
    }


def reference(xT, w1_words, w1_scales, w2_words, w2_scales, gate, offs, pos1, pos2, pos3, pos4):
    idx = unstriped(offs)
    w1 = np.stack([unpack_weight(w1_words[e], w1_scales[e], "e2m1") for e in range(E)])
    w2 = np.stack([unpack_weight(w2_words[e], w2_scales[e], "e2m1") for e in range(E)])
    xq = mxq(f64(xT)[:, idx], 0, "e4m3")
    h = gelu(by_expert(w1, xq))
    y = by_expert(w2, mxq(h, 0, "e4m3"))
    return sum(f64(gate[r]) * y[:, unstriped(p)] for r, p in enumerate((pos1, pos2, pos3, pos4)))

@@ -1,0 +1,264 @@
+from contextlib import ExitStack
+
+import concourse.mybir as mybir
+from concourse.masks import make_identity
+
+P = 128
+K, T, E, C, H, N = 512, 1024, 16, 256, 512, 128
+TOP = 4
+SLOTS = E * C
+FLOPS = 2 * SLOTS * (K * H + H * N)
+
+F32 = mybir.dt.float32
+BF16 = mybir.dt.bfloat16
+I32 = mybir.dt.int32
+U32 = mybir.dt.uint32
+U16 = mybir.dt.uint16
+U8 = mybir.dt.uint8
+FP8X4 = mybir.dt.float8_e4m3fn_x4
+FP4X4 = mybir.dt.float4_e2m1fn_x4
+COPY = mybir.ActivationFunctionType.Copy
+GELU = mybir.ActivationFunctionType.Gelu_apprx_tanh
+MULT = mybir.AluOpType.mult
+ADD = mybir.AluOpType.add
+
+X_CHUNKS = ((0, 512), (512, 256), (768, 256))
+X_PIECES = (((0, 256, "s"), (256, 256, "v")), ((0, 128, "s"), (128, 128, "v")), ((0, 128, "s"), (128, 128, "v")))
+GATHERS = tuple((e, 1) for e in range(E))
+SCALE_GROUPS = ((0, 4), (4, 12))
+WORD_GROUPS = ((0, 2), (2, 2), (4, 4), (8, 4), (12, 4))
+UNTANGLE_V = ()
+Y_COPY_V = (0, 2, 4)
+
+
+def tile_moe_tk_mlp_gelu_kernel(
+    tc, xT, w1_words, w1_scales, w2_words, w2_scales, gate, offs, pos1, pos2, pos3, pos4, out
+):
+    nc = tc.nc
+    with ExitStack() as ctx:
+        lists = ctx.enter_context(tc.tile_pool(name="lists", bufs=1))
+        held = ctx.enter_context(tc.tile_pool(name="held", bufs=1))
+        picked = ctx.enter_context(tc.tile_pool(name="picked", bufs=3))
+        turns = ctx.enter_context(tc.tile_pool(name="turns", bufs=1))
+        ring = ctx.enter_context(tc.tile_pool(name="ring", bufs=3))
+        a_psum = ctx.enter_context(tc.psum_pool(name="a_psum", bufs=4))
+        t_psum = ctx.enter_context(tc.psum_pool(name="t_psum", bufs=2))
+        y_psum = ctx.enter_context(tc.psum_pool(name="y_psum", bufs=2))
+
+        warm = held.tile([P, 1], F32, name="warm")
+        nc.vector.memset(warm[:], 0.0)
+        warm_out = held.tile([P, 1], F32, name="warm_out")
+        nc.scalar.activation(warm_out[:], warm[:], GELU)
+
+        w1_planes = []
+        for e0, n in SCALE_GROUPS:
+            plane = held.tile([P, n * H], U8, name=f"w1_planes{e0}", align_bytes=64)
+            w1_planes.append((e0, n, plane))
+        w2_planes = held.tile([P, E * N], U8, name="w2_planes", align_bytes=64)
+        x_scales = held.tile([P, T], U8, name="x_scales", align_bytes=64)
+        nc.gpsimd.memset(x_scales[:], 0)
+        nc.vector.memset(w1_planes[0][2][:].bitcast(I32), 0)
+        nc.vector.memset(w2_planes[:].bitcast(I32), 0)
+        nc.vector.memset(w1_planes[1][2][:].bitcast(I32), 0)
+        ident = held.tile([P, P], F32, name="ident")
+        make_identity(nc, ident[:])
+
+        x_rows = xT.rearrange("(p j) t -> p j t", j=4)
+        x_raw = turns.tile([P, 4, T], F32, name="x_raw", tag="big")
+        for c0, w in X_CHUNKS:
+            nc.sync.dma_start(out=x_raw[:, :, c0 : c0 + w], in_=x_rows[:, :, c0 : c0 + w])
+        offs_t = lists.tile([P, SLOTS // 16], U16, name="offs_t")
+        nc.sync.dma_start(offs_t[:], offs)
+
+        w1_t = []
+        for e0, n in WORD_GROUPS:
+            tile = held.tile([P, n * 2 * H], U8, name=f"w1_t{e0}", align_bytes=64)
+            w1_t.append((e0, n, tile))
+
+        def load_w1(group):
+            e0, n, tile = w1_t[group]
+            nc.sync.dma_start(
+                out=tile[:].bitcast(I32).rearrange("p (e b) -> p e b", e=n),
+                in_=w1_words[e0 : e0 + n, 0, :, :].bitcast(I32).rearrange("e p b -> p e b"),
+            )
+
+        def load_w1_scales(group):
+            e0, n, plane = w1_planes[group]
+            for q in range(4):
+                nc.sync.dma_start(
+                    out=plane[32 * q : 32 * q + 4, :].bitcast(I32).rearrange("r (e i) -> r e i", e=n),
+                    in_=w1_scales[e0 : e0 + n, 0, 4 * q : 4 * q + 4, :].bitcast(I32).rearrange("e r i -> r e i"),
+                )
+
+        load_w1_scales(0)
+        load_w1(0)
+        w2_t = held.tile([P, E * 2 * N], U8, name="w2_t", align_bytes=64)
+        nc.sync.dma_start(
+            out=w2_t[:].bitcast(I32).rearrange("p (e b) -> p e b", e=E),
+            in_=w2_words[:, 0, :, :].bitcast(I32).rearrange("e p b -> p e b"),
+        )
+        for q in range(4):
+            nc.sync.dma_start(
+                out=w2_planes[32 * q : 32 * q + 4, :].bitcast(I32).rearrange("r (e i) -> r e i", e=E),
+                in_=w2_scales[:, 0, 4 * q : 4 * q + 4, :].bitcast(I32).rearrange("e r i -> r e i"),
+            )
+        load_w1(1)
+        load_w1_scales(1)
+        load_w1(2)
+        load_w1(3)
+        load_w1(4)
+        pos_t = []
+        for r, pos in enumerate((pos1, pos2, pos3, pos4)):
+            tile = lists.tile([P, T // 16], U16, name=f"pos_t{r}")
+            nc.sync.dma_start(tile[:], pos)
+            pos_t.append(tile)
+
+        x_codes = held.tile([P, T], U32, name="x_codes", align_bytes=64)
+        for (c0, w), pieces in zip(X_CHUNKS, X_PIECES):
+            for p0, pw, engine in pieces:
+                xb = held.tile([P, pw, 4], BF16, name=f"xb{c0 + p0}", align_bytes=64)
+                src = x_raw[:, :, c0 + p0 : c0 + p0 + pw].rearrange("p j t -> p t j")
+                if engine == "s":
+                    nc.scalar.copy(xb[:], src)
+                else:
+                    nc.vector.tensor_copy(xb[:], src)
+                cols = slice(c0 + p0, c0 + p0 + pw)
+                nc.vector.quantize_mx(
+                    out=x_codes[:, cols].bitcast(FP8X4),
+                    scales=x_scales[:, cols],
+                    in_=xb[:].rearrange("p t j -> p (t j)"),
+                )
+
+        gate_t = turns.tile([P, TOP, T], F32, name="gate_t", tag="big")
+        nc.sync.dma_start(out=gate_t[:], in_=gate.rearrange("r p t -> p r t"))
+
+        gathered = {}
+
+        def gather(g):
+            e0, n = GATHERS[g]
+            words = picked.tile([P, n * C], U32, name="words", align_bytes=64)
+            scales = picked.tile([P, n * C], U8, name="scales", align_bytes=64)
+            lst = offs_t[:, e0 * C // 16 : (e0 + n) * C // 16]
+            nc.vector.tensor_copy(words[:], x_codes[:].indirect(lst))
+            nc.vector.tensor_copy(scales[:], x_scales[:].indirect(lst))
+            for i in range(n):
+                gathered[e0 + i] = (words, scales, i * C)
+
+        def find(groups, e):
+            for e0, n, tile in groups:
+                if e0 <= e < e0 + n:
+                    return tile, e - e0
+
+        a_of, hb_of, tr_of, h4_of, q_of, y_of = {}, {}, {}, {}, {}, {}
+
+        def mm1(e):
+            words, scales, off = gathered[e]
+            w_tile, wi = find(w1_t, e)
+            s_tile, si = find(w1_planes, e)
+            banks = []
+            for b in range(2):
+                a = a_psum.tile([P, H], F32, name="a")
+                cols = slice(off + b * P, off + (b + 1) * P)
+                nc.tensor.matmul_mx(
+                    out=a[:],
+                    lhsT=words[:, cols].bitcast(FP8X4),
+                    lhsT_scale=scales[:, cols],
+                    rhs=w_tile[:, wi * 2 * H : (wi + 1) * 2 * H].bitcast(FP4X4),
+                    rhs_scale=s_tile[:, si * H : (si + 1) * H],
+                    start=True,
+                    stop=True,
+                )
+                banks.append(a)
+            a_of[e] = banks
+
+        def act(e):
+            hb = ring.tile([P, 2, 2, P, 2], BF16, name="hb", align_bytes=64)
+            for b in range(2):
+                nc.scalar.activation(hb[:, b], a_of[e][b][:].rearrange("s (p u e) -> s u p e", u=2, e=2), GELU)
+            hb_of[e] = hb
+
+        def turn(e):
+            tr = t_psum.tile([P, 4 * P], F32, name="tr")
+            words = hb_of[e][:].rearrange("s b u p e -> s (b u p e)").bitcast(F32)
+            for i in range(4):
+                nc.tensor.transpose(tr[:, i * P : (i + 1) * P], words[:, i * P : (i + 1) * P], ident[:])
+            tr_of[e] = tr
+
+        def untangle(e):
+            h4 = ring.tile([P, C * 4], BF16, name="h4", align_bytes=64)
+            dst = h4[:].bitcast(F32).rearrange("p (b r u) -> p b r u", b=2, u=2)
+            src = tr_of[e][:].rearrange("p (b u r) -> p b r u", b=2, u=2)
+            if e in UNTANGLE_V:
+                nc.vector.tensor_copy(dst, src)
+            else:
+                nc.scalar.copy(dst, src)
+            h4_of[e] = h4
+
+        def quant(e):
+            codes = ring.tile([P, C], U32, name="h_codes", align_bytes=64)
+            scales = ring.tile([P, C], U8, name="h_scales", align_bytes=64)
+            nc.vector.quantize_mx(out=codes[:].bitcast(FP8X4), scales=scales[:], in_=h4_of[e][:])
+            q_of[e] = (codes, scales)
+
+        y = held.tile([P, SLOTS], F32, name="y")
+
+        def mm2(e):
+            if e % 2 == 0:
+                yb = y_psum.tile([P, 2 * C], F32, name="yb")
+                y_of[e // 2] = yb
+            codes, scales = q_of[e]
+            half = slice(e % 2 * C, (e % 2 + 1) * C)
+            nc.tensor.matmul_mx(
+                out=y_of[e // 2][:, half],
+                lhsT=w2_t[:, e * 2 * N : (e + 1) * 2 * N].bitcast(FP4X4),
+                lhsT_scale=w2_planes[:, e * N : (e + 1) * N],
+                rhs=codes[:].bitcast(FP8X4),
+                rhs_scale=scales[:],
+                start=True,
+                stop=True,
+            )
+
+        def leave(pair):
+            dst = y[:, pair * 2 * C : (pair + 1) * 2 * C]
+            if pair in Y_COPY_V:
+                nc.vector.tensor_copy(dst, y_of[pair][:])
+            else:
+                nc.scalar.copy(dst, y_of[pair][:])
+
+        starts = {e0: g for g, (e0, n) in enumerate(GATHERS)}
+        gather(0)
+        gather(1)
+        for s in range(E + 2):
+            if s + 2 in starts:
+                gather(starts[s + 2])
+            if s < E:
+                mm1(s)
+            if 1 <= s <= E:
+                turn(s - 1)
+            if s < E:
+                act(s)
+            if 1 <= s <= E:
+                untangle(s - 1)
+            if s >= 2:
+                quant(s - 2)
+                mm2(s - 2)
+                if s % 2 == 1:
+                    leave((s - 2) // 2)
+
+        HALF = T // 2
+        prods = {}
+        for h in range(2):
+            for r in range(TOP):
+                p = held.tile([P, HALF], F32, name=f"prod{h}_{r}")
+                cols = slice(h * HALF, (h + 1) * HALF)
+                nc.vector.tensor_tensor(
+                    p[:], y[:].indirect(pos_t[r][:, h * HALF // 16 : (h + 1) * HALF // 16]), gate_t[:, r, cols], MULT
+                )
+                prods[h, r] = p
+            s01 = held.tile([P, HALF], F32, name=f"s01_{h}")
+            nc.vector.tensor_tensor(s01[:], prods[h, 0][:], prods[h, 1][:], ADD)
+            s23 = held.tile([P, HALF], F32, name=f"s23_{h}")
+            nc.vector.tensor_tensor(s23[:], prods[h, 2][:], prods[h, 3][:], ADD)
+            total = held.tile([P, HALF], F32, name=f"total_{h}")
+            nc.vector.tensor_tensor(total[:], s01[:], s23[:], ADD)
+            nc.sync.dma_start(out=out[:, h * HALF : (h + 1) * HALF], in_=total[:])

@@ -28,7 +28,7 @@ GATHERS = tuple((e, 1) for e in range(E))
 SCALE_GROUPS = ((0, 4), (4, 12))
 WORD_GROUPS = ((0, 2), (2, 2), (4, 4), (8, 4), (12, 4))
 UNTANGLE_V = ()
-Y_COPY_V = (0, 2, 4)
+Y_COPY_V = (0, 1, 2, 3, 4, 5, 6)
 
 
 def tile_moe_tk_mlp_gelu_kernel(
@@ -40,7 +40,7 @@ def tile_moe_tk_mlp_gelu_kernel(
         held = ctx.enter_context(tc.tile_pool(name="held", bufs=1))
         picked = ctx.enter_context(tc.tile_pool(name="picked", bufs=3))
         turns = ctx.enter_context(tc.tile_pool(name="turns", bufs=1))
-        ring = ctx.enter_context(tc.tile_pool(name="ring", bufs=3))
+        ring = ctx.enter_context(tc.tile_pool(name="ring", bufs=4))
         a_psum = ctx.enter_context(tc.psum_pool(name="a_psum", bufs=4))
         t_psum = ctx.enter_context(tc.psum_pool(name="t_psum", bufs=2))
         y_psum = ctx.enter_context(tc.psum_pool(name="y_psum", bufs=2))
@@ -149,6 +149,7 @@ def tile_moe_tk_mlp_gelu_kernel(
                 if e0 <= e < e0 + n:
                     return tile, e - e0
 
+        y = held.tile([P, SLOTS], F32, name="y")
         a_of, hb_of, tr_of, h4_of, q_of, y_of = {}, {}, {}, {}, {}, {}
 
         def mm1(e):
@@ -177,6 +178,43 @@ def tile_moe_tk_mlp_gelu_kernel(
                 nc.scalar.activation(hb[:, b], a_of[e][b][:].rearrange("s (p u e) -> s u p e", u=2, e=2), GELU)
             hb_of[e] = hb
 
+        def turn_half(e, b):
+            tr = t_psum.tile([P, 4 * P], F32, name="tr")
+            words = hb_of[e][:].rearrange("s b u p e -> s (b u p e)").bitcast(F32)
+            for u in range(2):
+                i = 2 * b + u
+                nc.tensor.transpose(tr[:, u * P : (u + 1) * P], words[:, i * P : (i + 1) * P], ident[:])
+            return tr
+
+        def finish_last(e):
+            yb = y_of[e // 2]
+            for b in range(2):
+                tr = turn_half(e, b)
+                h4 = ring.tile([P, 2 * P, 2], BF16, name="h4", align_bytes=64)
+                dst = h4[:].rearrange("p c w -> p (c w)").bitcast(F32).rearrange("p (r u) -> p r u", u=2)
+                src = tr[:, 0 : 2 * P].rearrange("p (u r) -> p r u", u=2)
+                if b == 0:
+                    nc.scalar.copy(dst, src)
+                else:
+                    nc.vector.tensor_copy(dst, src)
+                codes = ring.tile([P, P], U32, name="h_codes", align_bytes=64)
+                scales = ring.tile([P, P], U8, name="h_scales", align_bytes=64)
+                nc.vector.quantize_mx(
+                    out=codes[:].bitcast(FP8X4), scales=scales[:], in_=h4[:].rearrange("p c w -> p (c w)")
+                )
+                cols = slice(C + b * P, C + (b + 1) * P)
+                nc.tensor.matmul_mx(
+                    out=yb[:, cols],
+                    lhsT=w2_t[:, e * 2 * N : (e + 1) * 2 * N].bitcast(FP4X4),
+                    lhsT_scale=w2_planes[:, e * N : (e + 1) * N],
+                    rhs=codes[:].bitcast(FP8X4),
+                    rhs_scale=scales[:],
+                    start=True,
+                    stop=True,
+                )
+                at = e * C + b * P
+                nc.vector.tensor_copy(y[:, at : at + P], yb[:, cols])
+
         def turn(e):
             tr = t_psum.tile([P, 4 * P], F32, name="tr")
             words = hb_of[e][:].rearrange("s b u p e -> s (b u p e)").bitcast(F32)
@@ -200,23 +238,22 @@ def tile_moe_tk_mlp_gelu_kernel(
             nc.vector.quantize_mx(out=codes[:].bitcast(FP8X4), scales=scales[:], in_=h4_of[e][:])
             q_of[e] = (codes, scales)
 
-        y = held.tile([P, SLOTS], F32, name="y")
-
         def mm2(e):
             if e % 2 == 0:
                 yb = y_psum.tile([P, 2 * C], F32, name="yb")
                 y_of[e // 2] = yb
             codes, scales = q_of[e]
             half = slice(e % 2 * C, (e % 2 + 1) * C)
-            nc.tensor.matmul_mx(
-                out=y_of[e // 2][:, half],
-                lhsT=w2_t[:, e * 2 * N : (e + 1) * 2 * N].bitcast(FP4X4),
-                lhsT_scale=w2_planes[:, e * N : (e + 1) * N],
-                rhs=codes[:].bitcast(FP8X4),
-                rhs_scale=scales[:],
-                start=True,
-                stop=True,
-            )
+            for again in range(2):
+                nc.tensor.matmul_mx(
+                    out=y_of[e // 2][:, half],
+                    lhsT=w2_t[:, e * 2 * N : (e + 1) * 2 * N].bitcast(FP4X4),
+                    lhsT_scale=w2_planes[:, e * N : (e + 1) * N],
+                    rhs=codes[:].bitcast(FP8X4),
+                    rhs_scale=scales[:],
+                    start=True,
+                    stop=True,
+                )
 
         def leave(pair):
             dst = y[:, pair * 2 * C : (pair + 1) * 2 * C]
@@ -228,22 +265,25 @@ def tile_moe_tk_mlp_gelu_kernel(
         starts = {e0: g for g, (e0, n) in enumerate(GATHERS)}
         gather(0)
         gather(1)
-        for s in range(E + 2):
+        for s in range(E + 1):
             if s + 2 in starts:
                 gather(starts[s + 2])
             if s < E:
                 mm1(s)
-            if 1 <= s <= E:
+            if 1 <= s < E:
                 turn(s - 1)
             if s < E:
                 act(s)
-            if 1 <= s <= E:
+            if 1 <= s < E:
                 untangle(s - 1)
-            if s >= 2:
+            if 2 <= s <= E:
                 quant(s - 2)
                 mm2(s - 2)
                 if s % 2 == 1:
                     leave((s - 2) // 2)
+            if s == E:
+                nc.vector.tensor_copy(y[:, (E - 2) * C : (E - 1) * C], y_of[E // 2 - 1][:, 0:C])
+                finish_last(E - 1)
 
         HALF = T // 2
         prods = {}

@@ -1,7 +1,6 @@
 from contextlib import ExitStack
 
 import concourse.mybir as mybir
-from concourse.masks import make_identity
 
 P = 128
 K, T, E, C, H, N = 512, 1024, 16, 256, 512, 128
@@ -23,12 +22,13 @@ MULT = mybir.AluOpType.mult
 ADD = mybir.AluOpType.add
 
 X_CHUNKS = ((0, 512), (512, 256), (768, 256))
-X_PIECES = (((0, 256, "s"), (256, 256, "v")), ((0, 128, "s"), (128, 128, "v")), ((0, 128, "s"), (128, 128, "v")))
-GATHERS = tuple((e, 1) for e in range(E))
+X_PIECES = (((0, 256, "s"), (256, 256, "v")), ((0, 128, "s"), (128, 128, "v")), ((0, 128, "v"), (128, 64, "s"), (192, 64, "v")))
+GATHERS = ((0, 1), (1, 1)) + tuple((e, 2) for e in range(2, E - 2, 2)) + ((E - 2, 1), (E - 1, 1))
 SCALE_GROUPS = ((0, 4), (4, 12))
 WORD_GROUPS = ((0, 2), (2, 2), (4, 4), (8, 4), (12, 4))
-UNTANGLE_V = ()
-Y_COPY_V = (0, 1, 2, 3, 4, 5, 6)
+LAG = 1
+LEAD = 4
+PERMS = ((0, 1), (1, 1)) + tuple((e, 2) for e in range(2, E, 2))
 
 
 def tile_moe_tk_mlp_gelu_kernel(
@@ -38,12 +38,11 @@ def tile_moe_tk_mlp_gelu_kernel(
     with ExitStack() as ctx:
         lists = ctx.enter_context(tc.tile_pool(name="lists", bufs=1))
         held = ctx.enter_context(tc.tile_pool(name="held", bufs=1))
-        picked = ctx.enter_context(tc.tile_pool(name="picked", bufs=3))
+        picked = ctx.enter_context(tc.tile_pool(name="picked", bufs=2))
+        permuted = ctx.enter_context(tc.tile_pool(name="permuted", bufs=2))
         turns = ctx.enter_context(tc.tile_pool(name="turns", bufs=1))
-        ring = ctx.enter_context(tc.tile_pool(name="ring", bufs=4))
-        a_psum = ctx.enter_context(tc.psum_pool(name="a_psum", bufs=4))
-        t_psum = ctx.enter_context(tc.psum_pool(name="t_psum", bufs=2))
-        y_psum = ctx.enter_context(tc.psum_pool(name="y_psum", bufs=2))
+        ring = ctx.enter_context(tc.tile_pool(name="ring", bufs=6))
+        banks = ctx.enter_context(tc.psum_pool(name="banks", bufs=8))
 
         warm = held.tile([P, 1], F32, name="warm")
         nc.vector.memset(warm[:], 0.0)
@@ -60,15 +59,13 @@ def tile_moe_tk_mlp_gelu_kernel(
         nc.vector.memset(w1_planes[0][2][:].bitcast(I32), 0)
         nc.vector.memset(w2_planes[:].bitcast(I32), 0)
         nc.vector.memset(w1_planes[1][2][:].bitcast(I32), 0)
-        ident = held.tile([P, P], F32, name="ident")
-        make_identity(nc, ident[:])
 
         x_rows = xT.rearrange("(p j) t -> p j t", j=4)
         x_raw = turns.tile([P, 4, T], F32, name="x_raw", tag="big")
-        for c0, w in X_CHUNKS:
+
+        def load_x(chunk):
+            c0, w = X_CHUNKS[chunk]
             nc.sync.dma_start(out=x_raw[:, :, c0 : c0 + w], in_=x_rows[:, :, c0 : c0 + w])
-        offs_t = lists.tile([P, SLOTS // 16], U16, name="offs_t")
-        nc.sync.dma_start(offs_t[:], offs)
 
         w1_t = []
         for e0, n in WORD_GROUPS:
@@ -90,8 +87,14 @@ def tile_moe_tk_mlp_gelu_kernel(
                     in_=w1_scales[e0 : e0 + n, 0, 4 * q : 4 * q + 4, :].bitcast(I32).rearrange("e r i -> r e i"),
                 )
 
+        load_x(0)
         load_w1_scales(0)
         load_w1(0)
+        load_x(1)
+        load_x(2)
+        offs_t = lists.tile([P, SLOTS // 16], U16, name="offs_t")
+        nc.sync.dma_start(offs_t[:], offs)
+        load_w1(1)
         w2_t = held.tile([P, E * 2 * N], U8, name="w2_t", align_bytes=64)
         nc.sync.dma_start(
             out=w2_t[:].bitcast(I32).rearrange("p (e b) -> p e b", e=E),
@@ -102,7 +105,6 @@ def tile_moe_tk_mlp_gelu_kernel(
                 out=w2_planes[32 * q : 32 * q + 4, :].bitcast(I32).rearrange("r (e i) -> r e i", e=E),
                 in_=w2_scales[:, 0, 4 * q : 4 * q + 4, :].bitcast(I32).rearrange("e r i -> r e i"),
             )
-        load_w1(1)
         load_w1_scales(1)
         load_w1(2)
         load_w1(3)
@@ -150,155 +152,138 @@ def tile_moe_tk_mlp_gelu_kernel(
                     return tile, e - e0
 
         y = held.tile([P, SLOTS], F32, name="y")
-        a_of, hb_of, tr_of, h4_of, q_of, y_of = {}, {}, {}, {}, {}, {}
+        bank_of, h4_of, q_of, w1p_of = {}, {}, {}, {}
+        BOTH = (0, 1)
+
+        w1_sp = held.tile([P, E * H], U8, name="w1_sp", align_bytes=64)
+
+        def permute_scales(e0, n):
+            s_tile, si = find(w1_planes, e0)
+            nc.gpsimd.tensor_copy(
+                w1_sp[:, e0 * H : (e0 + n) * H].rearrange("p (e t m) -> p e t m", e=n, t=4),
+                s_tile[:, si * H : (si + n) * H].rearrange("p (e m t) -> p e t m", e=n, t=4),
+            )
+
+        def permute_words(e0, n):
+            w_tile, wi = find(w1_t, e0)
+            w1p = permuted.tile([P, n * 2 * H], U8, name="w1p", align_bytes=64)
+            nc.vector.tensor_copy(
+                w1p[:].bitcast(U16).rearrange("p (e t m) -> p e t m", e=n, t=4),
+                w_tile[:, wi * 2 * H : (wi + n) * 2 * H].bitcast(U16).rearrange("p (e m t) -> p e t m", e=n, t=4),
+            )
+            for i in range(n):
+                w1p_of[e0 + i] = (w1p, i * 2 * H)
 
         def mm1(e):
             words, scales, off = gathered[e]
-            w_tile, wi = find(w1_t, e)
-            s_tile, si = find(w1_planes, e)
-            banks = []
+            w1p, at = w1p_of[e]
             for b in range(2):
-                a = a_psum.tile([P, H], F32, name="a")
+                bank = banks.tile([P, 4 * P], F32, name="bank")
                 cols = slice(off + b * P, off + (b + 1) * P)
-                nc.tensor.matmul_mx(
-                    out=a[:],
-                    lhsT=words[:, cols].bitcast(FP8X4),
-                    lhsT_scale=scales[:, cols],
-                    rhs=w_tile[:, wi * 2 * H : (wi + 1) * 2 * H].bitcast(FP4X4),
-                    rhs_scale=s_tile[:, si * H : (si + 1) * H],
-                    start=True,
-                    stop=True,
-                )
-                banks.append(a)
-            a_of[e] = banks
+                for t in range(4):
+                    nc.tensor.matmul_mx(
+                        out=bank[:, t * P : (t + 1) * P],
+                        lhsT=w1p[:, at + t * 2 * P : at + (t + 1) * 2 * P].bitcast(FP4X4),
+                        lhsT_scale=w1_sp[:, e * H + t * P : e * H + (t + 1) * P],
+                        rhs=words[:, cols].bitcast(FP8X4),
+                        rhs_scale=scales[:, cols],
+                        start=True,
+                        stop=True,
+                    )
+                bank_of[e, b] = bank
 
         def act(e):
-            hb = ring.tile([P, 2, 2, P, 2], BF16, name="hb", align_bytes=64)
-            for b in range(2):
-                nc.scalar.activation(hb[:, b], a_of[e][b][:].rearrange("s (p u e) -> s u p e", u=2, e=2), GELU)
-            hb_of[e] = hb
-
-        def turn_half(e, b):
-            tr = t_psum.tile([P, 4 * P], F32, name="tr")
-            words = hb_of[e][:].rearrange("s b u p e -> s (b u p e)").bitcast(F32)
-            for u in range(2):
-                i = 2 * b + u
-                nc.tensor.transpose(tr[:, u * P : (u + 1) * P], words[:, i * P : (i + 1) * P], ident[:])
-            return tr
-
-        def finish_last(e):
-            yb = y_of[e // 2]
-            for b in range(2):
-                tr = turn_half(e, b)
-                h4 = ring.tile([P, 2 * P, 2], BF16, name="h4", align_bytes=64)
-                dst = h4[:].rearrange("p c w -> p (c w)").bitcast(F32).rearrange("p (r u) -> p r u", u=2)
-                src = tr[:, 0 : 2 * P].rearrange("p (u r) -> p r u", u=2)
-                if b == 0:
-                    nc.scalar.copy(dst, src)
-                else:
-                    nc.vector.tensor_copy(dst, src)
-                codes = ring.tile([P, P], U32, name="h_codes", align_bytes=64)
-                scales = ring.tile([P, P], U8, name="h_scales", align_bytes=64)
-                nc.vector.quantize_mx(
-                    out=codes[:].bitcast(FP8X4), scales=scales[:], in_=h4[:].rearrange("p c w -> p (c w)")
-                )
-                cols = slice(C + b * P, C + (b + 1) * P)
-                nc.tensor.matmul_mx(
-                    out=yb[:, cols],
-                    lhsT=w2_t[:, e * 2 * N : (e + 1) * 2 * N].bitcast(FP4X4),
-                    lhsT_scale=w2_planes[:, e * N : (e + 1) * N],
-                    rhs=codes[:].bitcast(FP8X4),
-                    rhs_scale=scales[:],
-                    start=True,
-                    stop=True,
-                )
-                at = e * C + b * P
-                nc.vector.tensor_copy(y[:, at : at + P], yb[:, cols])
-
-        def turn(e):
-            tr = t_psum.tile([P, 4 * P], F32, name="tr")
-            words = hb_of[e][:].rearrange("s b u p e -> s (b u p e)").bitcast(F32)
-            for i in range(4):
-                nc.tensor.transpose(tr[:, i * P : (i + 1) * P], words[:, i * P : (i + 1) * P], ident[:])
-            tr_of[e] = tr
-
-        def untangle(e):
             h4 = ring.tile([P, C * 4], BF16, name="h4", align_bytes=64)
-            dst = h4[:].bitcast(F32).rearrange("p (b r u) -> p b r u", b=2, u=2)
-            src = tr_of[e][:].rearrange("p (b u r) -> p b r u", b=2, u=2)
-            if e in UNTANGLE_V:
-                nc.vector.tensor_copy(dst, src)
-            else:
-                nc.scalar.copy(dst, src)
+            for b in range(2):
+                nc.scalar.activation(
+                    h4[:, b * 4 * P : (b + 1) * 4 * P].rearrange("p (n t) -> p n t", t=4),
+                    bank_of[e, b][:].rearrange("p (t n) -> p n t", t=4),
+                    GELU,
+                )
             h4_of[e] = h4
 
-        def quant(e):
-            codes = ring.tile([P, C], U32, name="h_codes", align_bytes=64)
-            scales = ring.tile([P, C], U8, name="h_scales", align_bytes=64)
-            nc.vector.quantize_mx(out=codes[:].bitcast(FP8X4), scales=scales[:], in_=h4_of[e][:])
-            q_of[e] = (codes, scales)
+        def quant(e, blocks):
+            w = len(blocks) * P
+            codes = ring.tile([P, w], U32, name="h_codes", align_bytes=64)
+            scales = ring.tile([P, w], U8, name="h_scales", align_bytes=64)
+            at = blocks[0] * P * 4
+            nc.vector.quantize_mx(out=codes[:].bitcast(FP8X4), scales=scales[:], in_=h4_of[e][:, at : at + 4 * w])
+            q_of[e, blocks] = (codes, scales)
 
-        def mm2(e):
-            if e % 2 == 0:
-                yb = y_psum.tile([P, 2 * C], F32, name="yb")
-                y_of[e // 2] = yb
-            codes, scales = q_of[e]
-            half = slice(e % 2 * C, (e % 2 + 1) * C)
-            for again in range(2):
-                nc.tensor.matmul_mx(
-                    out=y_of[e // 2][:, half],
-                    lhsT=w2_t[:, e * 2 * N : (e + 1) * 2 * N].bitcast(FP4X4),
-                    lhsT_scale=w2_planes[:, e * N : (e + 1) * N],
-                    rhs=codes[:].bitcast(FP8X4),
-                    rhs_scale=scales[:],
-                    start=True,
-                    stop=True,
-                )
+        def mm2(e, blocks, bank, at):
+            codes, scales = q_of[e, blocks]
+            w = len(blocks) * P
+            nc.tensor.matmul_mx(
+                out=bank[:, at : at + w],
+                lhsT=w2_t[:, e * 2 * N : (e + 1) * 2 * N].bitcast(FP4X4),
+                lhsT_scale=w2_planes[:, e * N : (e + 1) * N],
+                rhs=codes[:].bitcast(FP8X4),
+                rhs_scale=scales[:],
+                start=True,
+                stop=True,
+            )
 
-        def leave(pair):
-            dst = y[:, pair * 2 * C : (pair + 1) * 2 * C]
-            if pair in Y_COPY_V:
-                nc.vector.tensor_copy(dst, y_of[pair][:])
+        def leave(copy, e, blocks, bank, at):
+            w = len(blocks) * P
+            to = e * C + blocks[0] * P
+            copy(y[:, to : to + w], bank[:, at : at + w])
+
+        def back(e):
+            if e + LAG < E:
+                bank = bank_of[e + LAG, 1]
             else:
-                nc.scalar.copy(dst, y_of[pair][:])
+                bank = banks.tile([P, 4 * P], F32, name="bank")
+            mm2(e, BOTH, bank, 0)
+            leave(nc.scalar.copy, e, BOTH, bank, 0)
 
+        perms = {e0: n for e0, n in PERMS}
         starts = {e0: g for g, (e0, n) in enumerate(GATHERS)}
-        gather(0)
-        gather(1)
-        for s in range(E + 1):
-            if s + 2 in starts:
-                gather(starts[s + 2])
-            if s < E:
-                mm1(s)
-            if 1 <= s < E:
-                turn(s - 1)
-            if s < E:
-                act(s)
-            if 1 <= s < E:
-                untangle(s - 1)
-            if 2 <= s <= E:
-                quant(s - 2)
-                mm2(s - 2)
-                if s % 2 == 1:
-                    leave((s - 2) // 2)
-            if s == E:
-                nc.vector.tensor_copy(y[:, (E - 2) * C : (E - 1) * C], y_of[E // 2 - 1][:, 0:C])
-                finish_last(E - 1)
+        for e in range(E):
+            permute_scales(e, 1)
+        permute_words(0, 1)
+        permute_words(1, 1)
+        for e in range(LEAD):
+            if e in starts:
+                gather(starts[e])
+            if e >= 2 and e in perms:
+                permute_words(e, perms[e])
+        for s in range(E):
+            mm1(s)
+            act(s)
+            if s < E - 1:
+                quant(s, BOTH)
+            if s >= LAG:
+                back(s - LAG)
+            if s + LEAD in starts:
+                gather(starts[s + LEAD])
+            if s + LEAD in perms:
+                permute_words(s + LEAD, perms[s + LEAD])
+        for e in range(E - LAG, E - 1):
+            back(e)
+        last = E - 1
+        end_bank = banks.tile([P, 4 * P], F32, name="bank")
+        for b in range(2):
+            quant(last, (b,))
+            mm2(last, (b,), end_bank, b * P)
+            leave(nc.vector.tensor_copy if b else nc.scalar.copy, last, (b,), end_bank, b * P)
 
-        HALF = T // 2
-        prods = {}
-        for h in range(2):
-            for r in range(TOP):
-                p = held.tile([P, HALF], F32, name=f"prod{h}_{r}")
-                cols = slice(h * HALF, (h + 1) * HALF)
-                nc.vector.tensor_tensor(
-                    p[:], y[:].indirect(pos_t[r][:, h * HALF // 16 : (h + 1) * HALF // 16]), gate_t[:, r, cols], MULT
-                )
-                prods[h, r] = p
-            s01 = held.tile([P, HALF], F32, name=f"s01_{h}")
-            nc.vector.tensor_tensor(s01[:], prods[h, 0][:], prods[h, 1][:], ADD)
-            s23 = held.tile([P, HALF], F32, name=f"s23_{h}")
-            nc.vector.tensor_tensor(s23[:], prods[h, 2][:], prods[h, 3][:], ADD)
-            total = held.tile([P, HALF], F32, name=f"total_{h}")
-            nc.vector.tensor_tensor(total[:], s01[:], s23[:], ADD)
-            nc.sync.dma_start(out=out[:, h * HALF : (h + 1) * HALF], in_=total[:])
+        prods = []
+
+        def product(r):
+            p = held.tile([P, T], F32, name=f"prod{r}")
+            nc.vector.tensor_tensor(p[:], y[:].indirect(pos_t[r][:]), gate_t[:, r, :], MULT)
+            prods.append(p)
+
+        s01 = held.tile([P, T], F32, name="s01")
+        s012 = held.tile([P, T], F32, name="s012")
+        product(0)
+        product(1)
+        product(2)
+        nc.vector.tensor_tensor(s01[:], prods[0][:], prods[1][:], ADD)
+        product(3)
+        nc.vector.tensor_tensor(s012[:], s01[:], prods[2][:], ADD)
+        for c0, w in ((0, 768), (768, 256)):
+            cols = slice(c0, c0 + w)
+            total = held.tile([P, w], F32, name=f"total{c0}")
+            nc.vector.tensor_tensor(total[:], s012[:, cols], prods[3][:, cols], ADD)
+            nc.sync.dma_start(out=out[:, cols], in_=total[:])

@@ -1,6 +1,7 @@
 from contextlib import ExitStack
 
 import concourse.mybir as mybir
+from concourse.masks import make_identity
 
 P = 128
 K, T, E, C, H, N = 512, 1024, 16, 256, 512, 128
@@ -26,9 +27,10 @@ X_PIECES = (((0, 256, "s"), (256, 256, "v")), ((0, 128, "s"), (128, 128, "v")), 
 GATHERS = ((0, 1), (1, 1)) + tuple((e, 2) for e in range(2, E - 2, 2)) + ((E - 2, 1), (E - 1, 1))
 SCALE_GROUPS = ((0, 4), (4, 12))
 WORD_GROUPS = ((0, 2), (2, 2), (4, 4), (8, 4), (12, 4))
-LAG = 1
+LAG = 6
 LEAD = 4
-PERMS = ((0, 1), (1, 1)) + tuple((e, 2) for e in range(2, E, 2))
+UNTANGLE_ON_VECTOR = (4, 8, 12)
+DIRECT = (E - 2, E - 1)
 
 
 def tile_moe_tk_mlp_gelu_kernel(
@@ -39,10 +41,10 @@ def tile_moe_tk_mlp_gelu_kernel(
         lists = ctx.enter_context(tc.tile_pool(name="lists", bufs=1))
         held = ctx.enter_context(tc.tile_pool(name="held", bufs=1))
         picked = ctx.enter_context(tc.tile_pool(name="picked", bufs=2))
-        permuted = ctx.enter_context(tc.tile_pool(name="permuted", bufs=2))
         turns = ctx.enter_context(tc.tile_pool(name="turns", bufs=1))
-        ring = ctx.enter_context(tc.tile_pool(name="ring", bufs=6))
-        banks = ctx.enter_context(tc.psum_pool(name="banks", bufs=8))
+        ring = ctx.enter_context(tc.tile_pool(name="ring", bufs=4))
+        banks = ctx.enter_context(tc.psum_pool(name="banks", bufs=5))
+        t_psum = ctx.enter_context(tc.psum_pool(name="t_psum", bufs=3))
 
         warm = held.tile([P, 1], F32, name="warm")
         nc.vector.memset(warm[:], 0.0)
@@ -59,13 +61,15 @@ def tile_moe_tk_mlp_gelu_kernel(
         nc.vector.memset(w1_planes[0][2][:].bitcast(I32), 0)
         nc.vector.memset(w2_planes[:].bitcast(I32), 0)
         nc.vector.memset(w1_planes[1][2][:].bitcast(I32), 0)
+        ident = held.tile([P, P], F32, name="ident")
+        make_identity(nc, ident[:])
 
         x_rows = xT.rearrange("(p j) t -> p j t", j=4)
         x_raw = turns.tile([P, 4, T], F32, name="x_raw", tag="big")
-
-        def load_x(chunk):
-            c0, w = X_CHUNKS[chunk]
+        for c0, w in X_CHUNKS:
             nc.sync.dma_start(out=x_raw[:, :, c0 : c0 + w], in_=x_rows[:, :, c0 : c0 + w])
+        offs_t = lists.tile([P, SLOTS // 16], U16, name="offs_t")
+        nc.sync.dma_start(offs_t[:], offs)
 
         w1_t = []
         for e0, n in WORD_GROUPS:
@@ -87,14 +91,8 @@ def tile_moe_tk_mlp_gelu_kernel(
                     in_=w1_scales[e0 : e0 + n, 0, 4 * q : 4 * q + 4, :].bitcast(I32).rearrange("e r i -> r e i"),
                 )
 
-        load_x(0)
         load_w1_scales(0)
         load_w1(0)
-        load_x(1)
-        load_x(2)
-        offs_t = lists.tile([P, SLOTS // 16], U16, name="offs_t")
-        nc.sync.dma_start(offs_t[:], offs)
-        load_w1(1)
         w2_t = held.tile([P, E * 2 * N], U8, name="w2_t", align_bytes=64)
         nc.sync.dma_start(
             out=w2_t[:].bitcast(I32).rearrange("p (e b) -> p e b", e=E),
@@ -105,6 +103,7 @@ def tile_moe_tk_mlp_gelu_kernel(
                 out=w2_planes[32 * q : 32 * q + 4, :].bitcast(I32).rearrange("r (e i) -> r e i", e=E),
                 in_=w2_scales[:, 0, 4 * q : 4 * q + 4, :].bitcast(I32).rearrange("e r i -> r e i"),
             )
+        load_w1(1)
         load_w1_scales(1)
         load_w1(2)
         load_w1(3)
@@ -138,13 +137,18 @@ def tile_moe_tk_mlp_gelu_kernel(
 
         def gather(g):
             e0, n = GATHERS[g]
-            words = picked.tile([P, n * C], U32, name="words", align_bytes=64)
-            scales = picked.tile([P, n * C], U8, name="scales", align_bytes=64)
-            lst = offs_t[:, e0 * C // 16 : (e0 + n) * C // 16]
-            nc.vector.tensor_copy(words[:], x_codes[:].indirect(lst))
-            nc.vector.tensor_copy(scales[:], x_scales[:].indirect(lst))
-            for i in range(n):
-                gathered[e0 + i] = (words, scales, i * C)
+            cuts = [(i * P, P) for i in range(2)] if g == 0 else [(0, n * C)]
+            for at, w in cuts:
+                pool = held if g == 0 else picked
+                words = pool.tile([P, w], U32, name=f"words{at}" if g == 0 else "words", align_bytes=64)
+                scales = pool.tile([P, w], U8, name=f"scales{at}" if g == 0 else "scales", align_bytes=64)
+                first = e0 * C + at
+                lst = offs_t[:, first // 16 : (first + w) // 16]
+                nc.vector.tensor_copy(words[:], x_codes[:].indirect(lst))
+                nc.vector.tensor_copy(scales[:], x_scales[:].indirect(lst))
+                for i in range(w // P):
+                    block = first // P + i
+                    gathered[block // 2, block % 2] = (words, scales, i * P)
 
         def find(groups, e):
             for e0, n, tile in groups:
@@ -152,61 +156,96 @@ def tile_moe_tk_mlp_gelu_kernel(
                     return tile, e - e0
 
         y = held.tile([P, SLOTS], F32, name="y")
-        bank_of, h4_of, q_of, w1p_of = {}, {}, {}, {}
+        bank_of, hb_of, tr_of, h4_of, q_of = {}, {}, {}, {}, {}
         BOTH = (0, 1)
 
-        w1_sp = held.tile([P, E * H], U8, name="w1_sp", align_bytes=64)
+        w1p = held.tile([P, len(DIRECT) * 2 * H], U8, name="w1p", align_bytes=64)
+        w1p_planes = held.tile([P, len(DIRECT) * H], U8, name="w1p_planes", align_bytes=64)
 
-        def permute_scales(e0, n):
+        def permute():
+            e0, n = DIRECT[0], len(DIRECT)
+            w_tile, wi = find(w1_t, e0)
             s_tile, si = find(w1_planes, e0)
             nc.gpsimd.tensor_copy(
-                w1_sp[:, e0 * H : (e0 + n) * H].rearrange("p (e t m) -> p e t m", e=n, t=4),
+                w1p_planes[:].rearrange("p (e t m) -> p e t m", e=n, t=4),
                 s_tile[:, si * H : (si + n) * H].rearrange("p (e m t) -> p e t m", e=n, t=4),
             )
-
-        def permute_words(e0, n):
-            w_tile, wi = find(w1_t, e0)
-            w1p = permuted.tile([P, n * 2 * H], U8, name="w1p", align_bytes=64)
             nc.vector.tensor_copy(
                 w1p[:].bitcast(U16).rearrange("p (e t m) -> p e t m", e=n, t=4),
                 w_tile[:, wi * 2 * H : (wi + n) * 2 * H].bitcast(U16).rearrange("p (e m t) -> p e t m", e=n, t=4),
             )
-            for i in range(n):
-                w1p_of[e0 + i] = (w1p, i * 2 * H)
 
         def mm1(e):
-            words, scales, off = gathered[e]
-            w1p, at = w1p_of[e]
+            w_tile, wi = find(w1_t, e)
+            s_tile, si = find(w1_planes, e)
             for b in range(2):
-                bank = banks.tile([P, 4 * P], F32, name="bank")
-                cols = slice(off + b * P, off + (b + 1) * P)
-                for t in range(4):
+                words, scales, off = gathered[e, b]
+                bank = banks.tile([P, H], F32, name="bank")
+                x_words = words[:, off : off + P].bitcast(FP8X4)
+                x_planes = scales[:, off : off + P]
+                if e in DIRECT:
+                    d = e - DIRECT[0]
+                    for t in range(4):
+                        at = d * H + t * P
+                        nc.tensor.matmul_mx(
+                            out=bank[:, t * P : (t + 1) * P],
+                            lhsT=w1p[:, 2 * at : 2 * at + 2 * P].bitcast(FP4X4),
+                            lhsT_scale=w1p_planes[:, at : at + P],
+                            rhs=x_words,
+                            rhs_scale=x_planes,
+                            start=True,
+                            stop=True,
+                        )
+                else:
                     nc.tensor.matmul_mx(
-                        out=bank[:, t * P : (t + 1) * P],
-                        lhsT=w1p[:, at + t * 2 * P : at + (t + 1) * 2 * P].bitcast(FP4X4),
-                        lhsT_scale=w1_sp[:, e * H + t * P : e * H + (t + 1) * P],
-                        rhs=words[:, cols].bitcast(FP8X4),
-                        rhs_scale=scales[:, cols],
+                        out=bank[:],
+                        lhsT=x_words,
+                        lhsT_scale=x_planes,
+                        rhs=w_tile[:, wi * 2 * H : (wi + 1) * 2 * H].bitcast(FP4X4),
+                        rhs_scale=s_tile[:, si * H : (si + 1) * H],
                         start=True,
                         stop=True,
                     )
                 bank_of[e, b] = bank
 
         def act(e):
+            if e in DIRECT:
+                h4 = ring.tile([P, C * 4], BF16, name="h4", align_bytes=64)
+                for b in range(2):
+                    nc.scalar.activation(
+                        h4[:, b * 4 * P : (b + 1) * 4 * P].rearrange("p (n t) -> p n t", t=4),
+                        bank_of[e, b][:].rearrange("p (t n) -> p n t", t=4),
+                        GELU,
+                    )
+                h4_of[e] = h4
+            else:
+                hb = ring.tile([P, 2, 2, P, 2], BF16, name="hb", align_bytes=64)
+                for b in range(2):
+                    nc.scalar.activation(hb[:, b], bank_of[e, b][:].rearrange("s (p u e) -> s u p e", u=2, e=2), GELU)
+                hb_of[e] = hb
+
+        def turn(e):
+            tr = t_psum.tile([P, 4 * P], F32, name="tr")
+            words = hb_of[e][:].rearrange("s b u p e -> s (b u p e)").bitcast(F32)
+            for i in range(4):
+                nc.tensor.transpose(tr[:, i * P : (i + 1) * P], words[:, i * P : (i + 1) * P], ident[:])
+            tr_of[e] = tr
+
+        def untangle(e):
             h4 = ring.tile([P, C * 4], BF16, name="h4", align_bytes=64)
-            for b in range(2):
-                nc.scalar.activation(
-                    h4[:, b * 4 * P : (b + 1) * 4 * P].rearrange("p (n t) -> p n t", t=4),
-                    bank_of[e, b][:].rearrange("p (t n) -> p n t", t=4),
-                    GELU,
-                )
+            dst = h4[:].bitcast(F32).rearrange("p (b r u) -> p b r u", b=2, u=2)
+            src = tr_of[e][:].rearrange("p (b u r) -> p b r u", b=2, u=2)
+            if e in UNTANGLE_ON_VECTOR:
+                nc.vector.tensor_copy(dst, src)
+            else:
+                nc.scalar.copy(dst, src)
             h4_of[e] = h4
 
         def quant(e, blocks):
             w = len(blocks) * P
+            at = blocks[0] * 4 * P
             codes = ring.tile([P, w], U32, name="h_codes", align_bytes=64)
             scales = ring.tile([P, w], U8, name="h_scales", align_bytes=64)
-            at = blocks[0] * P * 4
             nc.vector.quantize_mx(out=codes[:].bitcast(FP8X4), scales=scales[:], in_=h4_of[e][:, at : at + 4 * w])
             q_of[e, blocks] = (codes, scales)
 
@@ -232,36 +271,33 @@ def tile_moe_tk_mlp_gelu_kernel(
             if e + LAG < E:
                 bank = bank_of[e + LAG, 1]
             else:
-                bank = banks.tile([P, 4 * P], F32, name="bank")
+                bank = banks.tile([P, H], F32, name="bank")
             mm2(e, BOTH, bank, 0)
             leave(nc.scalar.copy, e, BOTH, bank, 0)
 
-        perms = {e0: n for e0, n in PERMS}
         starts = {e0: g for g, (e0, n) in enumerate(GATHERS)}
-        for e in range(E):
-            permute_scales(e, 1)
-        permute_words(0, 1)
-        permute_words(1, 1)
         for e in range(LEAD):
             if e in starts:
                 gather(starts[e])
-            if e >= 2 and e in perms:
-                permute_words(e, perms[e])
+        permute()
         for s in range(E):
             mm1(s)
+            if s >= 1 and s - 1 not in DIRECT:
+                turn(s - 1)
             act(s)
-            if s < E - 1:
+            if s >= 1 and s - 1 not in DIRECT:
+                untangle(s - 1)
+                quant(s - 1, BOTH)
+            if s == E - 2:
                 quant(s, BOTH)
             if s >= LAG:
                 back(s - LAG)
             if s + LEAD in starts:
                 gather(starts[s + LEAD])
-            if s + LEAD in perms:
-                permute_words(s + LEAD, perms[s + LEAD])
         for e in range(E - LAG, E - 1):
             back(e)
         last = E - 1
-        end_bank = banks.tile([P, 4 * P], F32, name="bank")
+        end_bank = banks.tile([P, H], F32, name="bank")
         for b in range(2):
             quant(last, (b,))
             mm2(last, (b,), end_bank, b * P)

from contextlib import ExitStack

import concourse.mybir as mybir
from concourse.masks import make_identity

P = 128
K, T, E, C, H, N = 512, 1024, 16, 256, 512, 128
TOP = 4
SLOTS = E * C
FLOPS = 2 * SLOTS * (K * H + H * N)

F32 = mybir.dt.float32
BF16 = mybir.dt.bfloat16
I32 = mybir.dt.int32
U32 = mybir.dt.uint32
U16 = mybir.dt.uint16
U8 = mybir.dt.uint8
FP8X4 = mybir.dt.float8_e4m3fn_x4
FP4X4 = mybir.dt.float4_e2m1fn_x4
COPY = mybir.ActivationFunctionType.Copy
GELU = mybir.ActivationFunctionType.Gelu_apprx_tanh
MULT = mybir.AluOpType.mult
ADD = mybir.AluOpType.add

X_CHUNKS = ((0, 512), (512, 256), (768, 256))
X_PIECES = (((0, 256, "s"), (256, 256, "v")), ((0, 128, "s"), (128, 128, "v")), ((0, 128, "v"), (128, 64, "s"), (192, 64, "v")))
GATHERS = ((0, 1), (1, 1)) + tuple((e, 2) for e in range(2, E - 2, 2)) + ((E - 2, 1), (E - 1, 1))
SCALE_GROUPS = ((0, 4), (4, 12))
WORD_GROUPS = ((0, 2), (2, 2), (4, 4), (8, 4), (12, 4))
LAG = 6
LEAD = 4
UNTANGLE_ON_VECTOR = (4, 8, 12)
DIRECT = (E - 2, E - 1)


def tile_moe_tk_mlp_gelu_kernel(
    tc, xT, w1_words, w1_scales, w2_words, w2_scales, gate, offs, pos1, pos2, pos3, pos4, out
):
    nc = tc.nc
    with ExitStack() as ctx:
        lists = ctx.enter_context(tc.tile_pool(name="lists", bufs=1))
        held = ctx.enter_context(tc.tile_pool(name="held", bufs=1))
        picked = ctx.enter_context(tc.tile_pool(name="picked", bufs=2))
        turns = ctx.enter_context(tc.tile_pool(name="turns", bufs=1))
        ring = ctx.enter_context(tc.tile_pool(name="ring", bufs=4))
        banks = ctx.enter_context(tc.psum_pool(name="banks", bufs=5))
        t_psum = ctx.enter_context(tc.psum_pool(name="t_psum", bufs=3))

        warm = held.tile([P, 1], F32, name="warm")
        nc.vector.memset(warm[:], 0.0)
        warm_out = held.tile([P, 1], F32, name="warm_out")
        nc.scalar.activation(warm_out[:], warm[:], GELU)

        w1_planes = []
        for e0, n in SCALE_GROUPS:
            plane = held.tile([P, n * H], U8, name=f"w1_planes{e0}", align_bytes=64)
            w1_planes.append((e0, n, plane))
        w2_planes = held.tile([P, E * N], U8, name="w2_planes", align_bytes=64)
        x_scales = held.tile([P, T], U8, name="x_scales", align_bytes=64)
        nc.gpsimd.memset(x_scales[:], 0)
        nc.vector.memset(w1_planes[0][2][:].bitcast(I32), 0)
        nc.vector.memset(w2_planes[:].bitcast(I32), 0)
        nc.vector.memset(w1_planes[1][2][:].bitcast(I32), 0)
        ident = held.tile([P, P], F32, name="ident")
        make_identity(nc, ident[:])

        x_rows = xT.rearrange("(p j) t -> p j t", j=4)
        x_raw = turns.tile([P, 4, T], F32, name="x_raw", tag="big")
        for c0, w in X_CHUNKS:
            nc.sync.dma_start(out=x_raw[:, :, c0 : c0 + w], in_=x_rows[:, :, c0 : c0 + w])
        offs_t = lists.tile([P, SLOTS // 16], U16, name="offs_t")
        nc.sync.dma_start(offs_t[:], offs)

        w1_t = []
        for e0, n in WORD_GROUPS:
            tile = held.tile([P, n * 2 * H], U8, name=f"w1_t{e0}", align_bytes=64)
            w1_t.append((e0, n, tile))

        def load_w1(group):
            e0, n, tile = w1_t[group]
            nc.sync.dma_start(
                out=tile[:].bitcast(I32).rearrange("p (e b) -> p e b", e=n),
                in_=w1_words[e0 : e0 + n, 0, :, :].bitcast(I32).rearrange("e p b -> p e b"),
            )

        def load_w1_scales(group):
            e0, n, plane = w1_planes[group]
            for q in range(4):
                nc.sync.dma_start(
                    out=plane[32 * q : 32 * q + 4, :].bitcast(I32).rearrange("r (e i) -> r e i", e=n),
                    in_=w1_scales[e0 : e0 + n, 0, 4 * q : 4 * q + 4, :].bitcast(I32).rearrange("e r i -> r e i"),
                )

        load_w1_scales(0)
        load_w1(0)
        w2_t = held.tile([P, E * 2 * N], U8, name="w2_t", align_bytes=64)
        nc.sync.dma_start(
            out=w2_t[:].bitcast(I32).rearrange("p (e b) -> p e b", e=E),
            in_=w2_words[:, 0, :, :].bitcast(I32).rearrange("e p b -> p e b"),
        )
        for q in range(4):
            nc.sync.dma_start(
                out=w2_planes[32 * q : 32 * q + 4, :].bitcast(I32).rearrange("r (e i) -> r e i", e=E),
                in_=w2_scales[:, 0, 4 * q : 4 * q + 4, :].bitcast(I32).rearrange("e r i -> r e i"),
            )
        load_w1(1)
        load_w1_scales(1)
        load_w1(2)
        load_w1(3)
        load_w1(4)
        pos_t = []
        for r, pos in enumerate((pos1, pos2, pos3, pos4)):
            tile = lists.tile([P, T // 16], U16, name=f"pos_t{r}")
            nc.sync.dma_start(tile[:], pos)
            pos_t.append(tile)

        x_codes = held.tile([P, T], U32, name="x_codes", align_bytes=64)
        for (c0, w), pieces in zip(X_CHUNKS, X_PIECES):
            for p0, pw, engine in pieces:
                xb = held.tile([P, pw, 4], BF16, name=f"xb{c0 + p0}", align_bytes=64)
                src = x_raw[:, :, c0 + p0 : c0 + p0 + pw].rearrange("p j t -> p t j")
                if engine == "s":
                    nc.scalar.copy(xb[:], src)
                else:
                    nc.vector.tensor_copy(xb[:], src)
                cols = slice(c0 + p0, c0 + p0 + pw)
                nc.vector.quantize_mx(
                    out=x_codes[:, cols].bitcast(FP8X4),
                    scales=x_scales[:, cols],
                    in_=xb[:].rearrange("p t j -> p (t j)"),
                )

        gate_t = turns.tile([P, TOP, T], F32, name="gate_t", tag="big")
        nc.sync.dma_start(out=gate_t[:], in_=gate.rearrange("r p t -> p r t"))

        gathered = {}

        def gather(g):
            e0, n = GATHERS[g]
            cuts = [(i * P, P) for i in range(2)] if g == 0 else [(0, n * C)]
            for at, w in cuts:
                pool = held if g == 0 else picked
                words = pool.tile([P, w], U32, name=f"words{at}" if g == 0 else "words", align_bytes=64)
                scales = pool.tile([P, w], U8, name=f"scales{at}" if g == 0 else "scales", align_bytes=64)
                first = e0 * C + at
                lst = offs_t[:, first // 16 : (first + w) // 16]
                nc.vector.tensor_copy(words[:], x_codes[:].indirect(lst))
                nc.vector.tensor_copy(scales[:], x_scales[:].indirect(lst))
                for i in range(w // P):
                    block = first // P + i
                    gathered[block // 2, block % 2] = (words, scales, i * P)

        def find(groups, e):
            for e0, n, tile in groups:
                if e0 <= e < e0 + n:
                    return tile, e - e0

        y = held.tile([P, SLOTS], F32, name="y")
        bank_of, hb_of, tr_of, h4_of, q_of = {}, {}, {}, {}, {}
        BOTH = (0, 1)

        w1p = held.tile([P, len(DIRECT) * 2 * H], U8, name="w1p", align_bytes=64)
        w1p_planes = held.tile([P, len(DIRECT) * H], U8, name="w1p_planes", align_bytes=64)

        def permute():
            e0, n = DIRECT[0], len(DIRECT)
            w_tile, wi = find(w1_t, e0)
            s_tile, si = find(w1_planes, e0)
            nc.gpsimd.tensor_copy(
                w1p_planes[:].rearrange("p (e t m) -> p e t m", e=n, t=4),
                s_tile[:, si * H : (si + n) * H].rearrange("p (e m t) -> p e t m", e=n, t=4),
            )
            nc.vector.tensor_copy(
                w1p[:].bitcast(U16).rearrange("p (e t m) -> p e t m", e=n, t=4),
                w_tile[:, wi * 2 * H : (wi + n) * 2 * H].bitcast(U16).rearrange("p (e m t) -> p e t m", e=n, t=4),
            )

        def mm1(e):
            w_tile, wi = find(w1_t, e)
            s_tile, si = find(w1_planes, e)
            for b in range(2):
                words, scales, off = gathered[e, b]
                bank = banks.tile([P, H], F32, name="bank")
                x_words = words[:, off : off + P].bitcast(FP8X4)
                x_planes = scales[:, off : off + P]
                if e in DIRECT:
                    d = e - DIRECT[0]
                    for t in range(4):
                        at = d * H + t * P
                        nc.tensor.matmul_mx(
                            out=bank[:, t * P : (t + 1) * P],
                            lhsT=w1p[:, 2 * at : 2 * at + 2 * P].bitcast(FP4X4),
                            lhsT_scale=w1p_planes[:, at : at + P],
                            rhs=x_words,
                            rhs_scale=x_planes,
                            start=True,
                            stop=True,
                        )
                else:
                    nc.tensor.matmul_mx(
                        out=bank[:],
                        lhsT=x_words,
                        lhsT_scale=x_planes,
                        rhs=w_tile[:, wi * 2 * H : (wi + 1) * 2 * H].bitcast(FP4X4),
                        rhs_scale=s_tile[:, si * H : (si + 1) * H],
                        start=True,
                        stop=True,
                    )
                bank_of[e, b] = bank

        def act(e):
            if e in DIRECT:
                h4 = ring.tile([P, C * 4], BF16, name="h4", align_bytes=64)
                for b in range(2):
                    nc.scalar.activation(
                        h4[:, b * 4 * P : (b + 1) * 4 * P].rearrange("p (n t) -> p n t", t=4),
                        bank_of[e, b][:].rearrange("p (t n) -> p n t", t=4),
                        GELU,
                    )
                h4_of[e] = h4
            else:
                hb = ring.tile([P, 2, 2, P, 2], BF16, name="hb", align_bytes=64)
                for b in range(2):
                    nc.scalar.activation(hb[:, b], bank_of[e, b][:].rearrange("s (p u e) -> s u p e", u=2, e=2), GELU)
                hb_of[e] = hb

        def turn(e):
            tr = t_psum.tile([P, 4 * P], F32, name="tr")
            words = hb_of[e][:].rearrange("s b u p e -> s (b u p e)").bitcast(F32)
            for i in range(4):
                nc.tensor.transpose(tr[:, i * P : (i + 1) * P], words[:, i * P : (i + 1) * P], ident[:])
            tr_of[e] = tr

        def untangle(e):
            h4 = ring.tile([P, C * 4], BF16, name="h4", align_bytes=64)
            dst = h4[:].bitcast(F32).rearrange("p (b r u) -> p b r u", b=2, u=2)
            src = tr_of[e][:].rearrange("p (b u r) -> p b r u", b=2, u=2)
            if e in UNTANGLE_ON_VECTOR:
                nc.vector.tensor_copy(dst, src)
            else:
                nc.scalar.copy(dst, src)
            h4_of[e] = h4

        def quant(e, blocks):
            w = len(blocks) * P
            at = blocks[0] * 4 * P
            codes = ring.tile([P, w], U32, name="h_codes", align_bytes=64)
            scales = ring.tile([P, w], U8, name="h_scales", align_bytes=64)
            nc.vector.quantize_mx(out=codes[:].bitcast(FP8X4), scales=scales[:], in_=h4_of[e][:, at : at + 4 * w])
            q_of[e, blocks] = (codes, scales)

        def mm2(e, blocks, bank, at):
            codes, scales = q_of[e, blocks]
            w = len(blocks) * P
            nc.tensor.matmul_mx(
                out=bank[:, at : at + w],
                lhsT=w2_t[:, e * 2 * N : (e + 1) * 2 * N].bitcast(FP4X4),
                lhsT_scale=w2_planes[:, e * N : (e + 1) * N],
                rhs=codes[:].bitcast(FP8X4),
                rhs_scale=scales[:],
                start=True,
                stop=True,
            )

        def leave(copy, e, blocks, bank, at):
            w = len(blocks) * P
            to = e * C + blocks[0] * P
            copy(y[:, to : to + w], bank[:, at : at + w])

        def back(e):
            if e + LAG < E:
                bank = bank_of[e + LAG, 1]
            else:
                bank = banks.tile([P, H], F32, name="bank")
            mm2(e, BOTH, bank, 0)
            leave(nc.scalar.copy, e, BOTH, bank, 0)

        starts = {e0: g for g, (e0, n) in enumerate(GATHERS)}
        for e in range(LEAD):
            if e in starts:
                gather(starts[e])
        permute()
        for s in range(E):
            mm1(s)
            if s >= 1 and s - 1 not in DIRECT:
                turn(s - 1)
            act(s)
            if s >= 1 and s - 1 not in DIRECT:
                untangle(s - 1)
                quant(s - 1, BOTH)
            if s == E - 2:
                quant(s, BOTH)
            if s >= LAG:
                back(s - LAG)
            if s + LEAD in starts:
                gather(starts[s + LEAD])
        for e in range(E - LAG, E - 1):
            back(e)
        last = E - 1
        end_bank = banks.tile([P, H], F32, name="bank")
        for b in range(2):
            quant(last, (b,))
            mm2(last, (b,), end_bank, b * P)
            leave(nc.vector.tensor_copy if b else nc.scalar.copy, last, (b,), end_bank, b * P)

        prods = []

        def product(r):
            p = held.tile([P, T], F32, name=f"prod{r}")
            nc.vector.tensor_tensor(p[:], y[:].indirect(pos_t[r][:]), gate_t[:, r, :], MULT)
            prods.append(p)

        s01 = held.tile([P, T], F32, name="s01")
        s012 = held.tile([P, T], F32, name="s012")
        product(0)
        product(1)
        product(2)
        nc.vector.tensor_tensor(s01[:], prods[0][:], prods[1][:], ADD)
        product(3)
        nc.vector.tensor_tensor(s012[:], s01[:], prods[2][:], ADD)
        for c0, w in ((0, 768), (768, 256)):
            cols = slice(c0, c0 + w)
            total = held.tile([P, w], F32, name=f"total{c0}")
            nc.vector.tensor_tensor(total[:], s012[:, cols], prods[3][:, cols], ADD)
            nc.sync.dma_start(out=out[:, cols], in_=total[:])
